import numpy as np
import ml_dtypes


def mxq(x, axis, fmt="e4m3"):
    dtype, down = {"e4m3": (ml_dtypes.float8_e4m3fn, 7), "e5m2": (ml_dtypes.float8_e5m2, 14)}[fmt]
    v = np.moveaxis(np.asarray(x, np.float32).astype(ml_dtypes.bfloat16).astype(np.float64), axis, -1)
    blocks = v.reshape(v.shape[:-1] + (-1, 32))
    amax = np.abs(blocks).max(-1, keepdims=True)
    byte = np.maximum(np.where(amax > 0, np.frexp(amax)[1] - 1 + 127, 0) - down, 1)
    scale = np.exp2(byte - 127.0)
    codes = (blocks / scale).astype(np.float32).astype(dtype).astype(np.float64)
    return np.moveaxis((codes * scale).reshape(v.shape), -1, axis)


WIDE = False


def mx_kscale(k):
    if not WIDE:
        return np.ones(k)
    levels = np.array([10, -10, 5, -5, 0])
    if k % 512:
        return np.exp2(np.random.permutation(np.resize(levels, k // 32))).repeat(32)
    a = np.empty((k // 512, 16))
    for p in range(k // 512):
        a[p, :8] = np.random.permutation(np.resize(levels, 8))
        for g in range(8):
            far = levels[np.abs(levels - a[p, g]) >= 10]
            a[p, g + 8] = far[np.random.randint(len(far))]
    return np.exp2(a.ravel()).repeat(32)


def f64(x):
    return np.asarray(x).astype(np.float64)


def striped(idx):
    return np.tile(idx.reshape(-1, 16).T, (8, 1)).astype(np.uint16)


def unstriped(offs):
    return offs[:16].T.reshape(-1).astype(np.int64)


def pack_weight(w):
    k, n = w.shape
    w = f64(np.asarray(w, np.float32).astype(ml_dtypes.bfloat16)).reshape(k // 32, 32, n)
    amax = np.abs(w).max(1)
    byte = np.clip(np.where(amax > 0, np.frexp(amax)[1] - 1 + 127 - 7, 1), 1, 254)
    scaled = (w * np.exp2(127.0 - byte)[:, None, :]).reshape(k, n).astype(np.float32)
    words = np.ascontiguousarray(scaled.reshape(k // 512, 128, 4, n).transpose(0, 1, 3, 2)).astype(ml_dtypes.float8_e4m3fn).view(np.uint8)
    return words, np.ascontiguousarray(byte.astype(np.uint8).reshape(k // 512, 16, n))


def unpack_weight(words, scales):
    g, p, n, _ = words.shape
    vals = np.ascontiguousarray(words).view(ml_dtypes.float8_e4m3fn).astype(np.float64) * np.repeat(np.exp2(scales.astype(np.float64) - 127.0), 8, axis=1)[..., None]
    return vals.transpose(0, 1, 3, 2).reshape(g * 512, n)


E2M1 = np.array([0.0, 0.5, 1.0, 1.5, 2.0, 3.0, 4.0, 6.0, -0.0, -0.5, -1.0, -1.5, -2.0, -3.0, -4.0, -6.0])


def pack_fp4(w):
    k, n = w.shape
    w = f64(np.asarray(w, np.float32).astype(ml_dtypes.bfloat16)).reshape(k // 32, 32, n)
    amax = np.abs(w).max(1)
    mant, ex = np.frexp(amax / 6.0)
    byte = np.clip(np.where(amax > 0, np.where(mant > 0.5, ex, ex - 1) + 127, 1), 1, 254)
    scaled = (w * np.exp2(127.0 - byte)[:, None, :]).reshape(k, n).astype(np.float32)
    c = np.ascontiguousarray(scaled.reshape(k // 512, 128, 4, n).transpose(0, 1, 3, 2)).astype(ml_dtypes.float4_e2m1fn).view(np.uint8) & 0xF
    words = (c[..., 0::2] | (c[..., 1::2] << 4)).reshape(k // 512, 128, 2 * n)
    return np.ascontiguousarray(words), np.ascontiguousarray(byte.astype(np.uint8).reshape(k // 512, 16, n))


def unpack_fp4(words, scales):
    g, _, n = scales.shape
    words = np.ascontiguousarray(words).reshape(g, 128, n, 2)
    nib = np.empty((g, 128, n, 4), np.uint8)
    nib[..., 0::2] = words & 0xF
    nib[..., 1::2] = words >> 4
    vals = E2M1[nib] * np.repeat(np.exp2(scales.astype(np.float64) - 127.0), 8, axis=1)[..., None]
    return vals.transpose(0, 1, 3, 2).reshape(g * 512, n)


def sigmoid(v):
    return 1.0 / (1.0 + np.exp(-np.maximum(v, -700.0)))


K, T, S, D, N, H, V, U = 1024, 2048, 1024, 4, 256, 512, 256, 512


def setup_inputs():
    n = np.random.standard_normal
    s = mx_kscale(K)[:, None]
    u = mx_kscale(H)
    packed_xT = pack_weight(n((K, T)) * s)
    packed_w1 = pack_fp4(n((K, H)) / np.sqrt(K) / s)
    packed_w2 = pack_fp4(n((K, H)) / np.sqrt(K) / s)
    packed_w3 = pack_fp4(n((H, N)) / np.sqrt(H) / u[:, None])
    return {
        "x_words": packed_xT[0],
        "x_scales": packed_xT[1],
        "w1_words": packed_w1[0],
        "w1_scales": packed_w1[1],
        "w2_words": packed_w2[0],
        "w2_scales": packed_w2[1],
        "cost": (np.random.uniform(0.2, 0.9, (H, U))).astype(np.float32),
        "unit": (np.random.uniform(0.6, 1.4, (H, 1)) * u[:, None]).astype(np.float32),
        "w3_words": packed_w3[0],
        "w3_scales": packed_w3[1],
        "offs": striped(np.random.permutation(T)[:S]),
        "bud": striped(np.random.permutation(np.concatenate([np.arange(V), np.random.randint(0, V, U - V)]))),
    }


def reference(x_words, x_scales, w1_words, w1_scales, w2_words, w2_scales, cost, unit, w3_words, w3_scales, offs, bud):
    xq = unpack_weight(x_words, x_scales)[:, unstriped(offs)]
    en = unpack_fp4(w2_words, w2_scales).T @ xq
    ent = np.log(np.exp(en) + 1.0)
    lg = unpack_fp4(w1_words, w1_scales).T @ xq
    acc_ = np.exp(-1.0 * ent) * sigmoid(lg)
    two = acc_ * (np.pad(acc_, ((0, 0), (0, 1)))[:, 1:])
    gain = two.reshape(len(two), -1, D).sum(axis=2)
    gb = gain[:, unstriped(bud)]
    tree = ent.reshape(len(ent), -1, D).mean(axis=2)
    hid = f64(unit) * (gb / (f64(cost) + tree[:, unstriped(bud)] + 0.3))
    return unpack_fp4(w3_words, w3_scales).T @ mxq(hid, 0, "e4m3")

@@ -1,0 +1,269 @@
+import math
+from contextlib import ExitStack
+
+import concourse.mybir as mybir
+from concourse.masks import make_identity
+
+K, T, S, H, N, V, U = 1024, 2048, 1024, 512, 256, 256, 512
+FLOPS = 2 * (2 * K * H * S + H * N * U)
+
+F32 = mybir.dt.float32
+BF16 = mybir.dt.bfloat16
+I32 = mybir.dt.int32
+U32 = mybir.dt.uint32
+U16 = mybir.dt.uint16
+U8 = mybir.dt.uint8
+FP8X4 = mybir.dt.float8_e4m3fn_x4
+FP4X4 = mybir.dt.float4_e2m1fn_x4
+ALU = mybir.AluOpType
+ACT = mybir.ActivationFunctionType
+
+P = 128
+PASSES = K // 512
+TILES = H // P
+GROUP = 4
+CHUNK = 512
+CHUNKS = S // CHUNK
+HALF = 256
+WINDOW = V + 16
+KNEE = 11.0
+KNEE_SIGMOID = 1.0 / (1.0 + math.exp(KNEE))
+
+
+def tile_picked_yentrd_rel_p_kernel(
+    tc, x_words, x_scales, w1_words, w1_scales, w2_words, w2_scales, cost, unit, w3_words, w3_scales, offs, bud, out
+):
+    nc = tc.nc
+    with ExitStack() as ctx:
+        keep = ctx.enter_context(tc.tile_pool(name="keep", bufs=1))
+        reuse = ctx.enter_context(tc.tile_pool(name="reuse", bufs=1))
+        psum = ctx.enter_context(tc.psum_pool(name="psum", bufs=8))
+
+        def sb(shape, dtype, name):
+            return keep.tile(shape, dtype, name=name, align_bytes=64)
+
+        def bank(name):
+            return psum.tile([P, 512], F32, name=name, tag="bank")
+
+        offs_t = sb([P, S // 16], U16, "offs_t")
+        bud_t = sb([P, U // 16], U16, "bud_t")
+        xs_win = reuse.tile([P, T], U8, name="xs_win", align_bytes=64, offset=7680)
+        xw_win = [sb([P, T], I32, "xw_win%d" % o) for o in range(PASSES)]
+        xs_got = sb([P, S], U8, "xs_got")
+        xs_moved = sb([P, S], U8, "xs_moved")
+        xw_got = [[sb([P, CHUNK], U32, "xw_got%d_%d" % (o, c)) for c in range(CHUNKS)] for o in range(PASSES)]
+        w_w = [
+            reuse.tile([P, PASSES, 2 * H], U8, name="w_w0", align_bytes=64, offset=8768),
+            sb([P, PASSES, 2 * H], U8, "w_w1"),
+        ]
+        w_s = [sb([P, PASSES, H], U8, "w_s%d" % m) for m in range(2)]
+        w3_w = reuse.tile([P, 2 * N], U8, name="w3_w", align_bytes=64, offset=8192)
+        w3_s = sb([P, 1, N], U8, "w3_s")
+        cost_t = reuse.tile([P, TILES, U], F32, name="cost_t", align_bytes=64, offset=0)
+        unit_t = reuse.tile([P, TILES], F32, name="unit_t", align_bytes=64, offset=8704)
+        ident = sb([P, P], F32, "ident")
+
+        s_pair = [sb([P, 2, GROUP, V], F32, "s_pair%d" % t) for t in range(TILES // 2)]
+        s_t = [s_pair[t // 2][:, t % 2] for t in range(TILES)]
+        g_t = [sb([P, GROUP, V], F32, "g_t%d" % t) for t in range(TILES)]
+        a_t = [sb([P, GROUP, V + 8], F32, "a_t%d" % t) for t in range(TILES)]
+        over = [sb([P, V], F32, "over%d" % t) for t in range(TILES)]
+        prod = sb([P, TILES, V], F32, "prod")
+        logp = sb([P, TILES, V], F32, "logp")
+        tree_win = [sb([P, WINDOW], F32, "tree_win%d" % t) for t in range(TILES)]
+        gain_win = [sb([P, WINDOW], F32, "gain_win%d" % t) for t in range(TILES)]
+
+        nc.vector.memset(xs_win[:].bitcast(I32), 0)
+        nc.vector.memset(xs_moved[:].bitcast(I32), 0)
+
+        def load_scales(tile, scales):
+            nc.gpsimd.memset(tile[:].bitcast(I32), 0)
+            for q in range(4):
+                nc.gpsimd.dma_start(
+                    out=tile[32 * q : 32 * q + 4].bitcast(I32),
+                    in_=scales[:, 4 * q : 4 * q + 4, :].rearrange("o r c -> r o c").bitcast(I32),
+                )
+
+        nc.sync.dma_start(offs_t[:], offs)
+        for q in range(4):
+            nc.sync.dma_start(
+                out=xs_win[32 * q : 32 * q + 8, :].bitcast(I32), in_=x_scales[:, 4 * q : 4 * q + 4, :].bitcast(I32)
+            )
+        for o in range(PASSES):
+            nc.sync.dma_start(out=xw_win[o][:], in_=x_words[o].rearrange("p n t -> p (n t)").bitcast(I32))
+        nc.sync.dma_start(out=w_w[1][:].bitcast(I32), in_=w2_words.rearrange("o p c -> p o c").bitcast(I32))
+        nc.sync.dma_start(bud_t[:], bud)
+        load_scales(w_s[1], w2_scales)
+        load_scales(w_s[0], w1_scales)
+        load_scales(w3_s, w3_scales)
+        make_identity(nc, ident[:])
+        for t in range(TILES):
+            nc.gpsimd.memset(a_t[t][:, 0, V : V + 8], 0.0)
+            nc.gpsimd.memset(tree_win[t][:, V:WINDOW], 0.0)
+            nc.gpsimd.memset(gain_win[t][:, V:WINDOW], 0.0)
+
+        nc.vector.tensor_copy(xs_got[:], xs_win[:].indirect(offs_t[:]))
+        for q in range(4):
+            nc.scalar.dma_start(
+                out=xs_moved[32 * q : 32 * q + 4, :].bitcast(I32), in_=xs_got[32 * q + 4 : 32 * q + 8, :].bitcast(I32)
+            )
+        for o in range(PASSES):
+            for c in range(CHUNKS):
+                cols = slice(c * CHUNK // 16, (c + 1) * CHUNK // 16)
+                nc.vector.tensor_copy(xw_got[o][c][:], xw_win[o][:].bitcast(U32).indirect(offs_t[:, cols]))
+
+        nc.sync.dma_start(out=w_w[0][:].bitcast(I32), in_=w1_words.rearrange("o p c -> p o c").bitcast(I32))
+        with nc.allow_non_contiguous_dma(reason="one value a partition and tile"):
+            nc.sync.dma_start(out=unit_t[:], in_=unit.rearrange("(t p) o -> p (t o)", p=P))
+        nc.sync.dma_start(out=cost_t[:], in_=cost.rearrange("(t p) r -> p t r", p=P))
+        nc.sync.dma_start(out=w3_w[:].bitcast(I32), in_=w3_words[0].bitcast(I32))
+
+        def product(m, t, c):
+            acc = bank("acc")
+            for o in range(PASSES):
+                x_plane = xs_got if o == 0 else xs_moved
+                nc.tensor.matmul_mx(
+                    out=acc[:],
+                    lhsT=w_w[m][:, o, 2 * P * t : 2 * P * (t + 1)].bitcast(FP4X4),
+                    lhsT_scale=w_s[m][:, o, P * t : P * (t + 1)],
+                    rhs=xw_got[o][c][:].bitcast(FP8X4),
+                    rhs_scale=x_plane[:, CHUNK * c : CHUNK * (c + 1)],
+                    start=(o == 0),
+                    stop=(o == PASSES - 1),
+                )
+            return acc[:].rearrange("p (v d) -> p d v", d=GROUP)
+
+        def entropy(c):
+            vs = slice(P * c, P * (c + 1))
+            en = []
+            for t in range(TILES):
+                en.append(product(1, t, c))
+                nc.scalar.activation(s_t[t][:, :, vs], en[t], ACT.Sigmoid, scale=-1.0)
+            for t in range(TILES):
+                nc.vector.tensor_scalar(over[t][:, vs], en[t][:, 0, :], KNEE, -GROUP * KNEE, ALU.max, ALU.add)
+            for d in range(1, GROUP):
+                for t in range(TILES):
+                    nc.vector.scalar_tensor_tensor(
+                        over[t][:, vs], en[t][:, d, :], KNEE, over[t][:, vs], ALU.max, ALU.add
+                    )
+
+        def logit(t, c):
+            lg = product(0, t, c)
+            nc.scalar.activation(g_t[t][:, :, P * c : P * (c + 1)], lg, ACT.Sigmoid)
+
+        def group_products():
+            for i in range(2):
+                nc.vector.tensor_scalar(
+                    prod[:, 2 * i : 2 * i + 2, :], s_pair[i][:, :, 0, :], KNEE_SIGMOID, None, ALU.max
+                )
+            for d in range(1, GROUP):
+                for i in range(2):
+                    both_tiles = prod[:, 2 * i : 2 * i + 2, :]
+                    nc.vector.scalar_tensor_tensor(
+                        both_tiles, s_pair[i][:, :, d, :], KNEE_SIGMOID, both_tiles, ALU.max, ALU.mult
+                    )
+
+        def gain(t):
+            a = a_t[t]
+            pair = sb([P, 2, V], F32, "pair%d" % t)
+            both = sb([P, 2, V], F32, "both%d" % t)
+            nc.vector.tensor_tensor(a[:, :, 0:V], s_t[t], g_t[t][:], ALU.mult)
+            nc.vector.tensor_tensor(pair[:, 0, :], a[:, 0, 0:V], a[:, 2, 0:V], ALU.add)
+            nc.vector.tensor_tensor(pair[:, 1, :], a[:, 0, 1 : V + 1], a[:, 2, 0:V], ALU.add)
+            nc.vector.scalar_tensor_tensor(both[:], a[:, 1::2, 0:V], unit_t[:, t : t + 1], pair[:], ALU.mult, ALU.mult)
+            nc.vector.tensor_tensor(gain_win[t][:, 0:V], both[:, 0, :], both[:, 1, :], ALU.add)
+
+        for c in range(CHUNKS):
+            entropy(c)
+        for t in range(TILES):
+            for c in range(CHUNKS):
+                logit(t, c)
+        group_products()
+        nc.scalar.activation(logp[:], prod[:], ACT.Ln)
+        for t in range(TILES):
+            nc.vector.tensor_tensor(tree_win[t][:, 0:V], over[t][:], logp[:, t, :], ALU.subtract)
+
+        def bud_cols(h):
+            return bud_t[:, h * HALF // 16 : (h + 1) * HALF // 16]
+
+        den = []
+        for h in range(2):
+            got = []
+            for t in range(TILES):
+                tree_got = sb([P, HALF], F32, "tree_got%d_%d" % (h, t))
+                nc.scalar.activation(
+                    tree_got[:], tree_win[t][:].indirect(bud_cols(h)), ACT.Copy, bias=0.3, scale=1.0 / GROUP
+                )
+                got.append(tree_got)
+            for j in range(2):
+                b = 2 * h + j
+                d_ps = bank("d_ps")
+                for t in range(TILES):
+                    cols = slice(P * t, P * (t + 1))
+                    nc.tensor.matmul(
+                        d_ps[:, cols], cost_t[:, t, P * b : P * (b + 1)], ident[:], start=True, stop=False,
+                        is_transpose=True,
+                    )
+                    nc.tensor.matmul(
+                        d_ps[:, cols], got[t][:, P * j : P * (j + 1)], ident[:], start=False, stop=True,
+                        is_transpose=True,
+                    )
+                den.append(d_ps)
+
+        gain_got = [[None] * TILES for h in range(2)]
+        for t in range(TILES):
+            gain(t)
+            for h in range(2):
+                fetched = sb([P, HALF], F32, "gain_got%d_%d" % (h, t))
+                if t == 0:
+                    nc.scalar.activation(fetched[:], gain_win[t][:].indirect(bud_cols(h)), ACT.Copy)
+                else:
+                    nc.vector.tensor_copy(fetched[:], gain_win[t][:].indirect(bud_cols(h)))
+                gain_got[h][t] = fetched
+
+        inv = []
+        for b in range(4):
+            sq = sb([P, H], F32, "sq%d" % b)
+            ra = sb([P, H], F32, "ra%d" % b)
+            q2 = sb([P, H], F32, "q2%d" % b)
+            w = sb([P, H], F32, "inv%d" % b)
+            nc.scalar.activation(sq[:], den[b][:], ACT.Square)
+            nc.scalar.activation(ra[:], sq[:], ACT.Abs_reciprocal_sqrt)
+            nc.scalar.activation(q2[:], ra[:], ACT.Square)
+            nc.vector.tensor_tensor(w[:], den[b][:], q2[:], ALU.mult)
+            inv.append(w)
+
+        for h in range(2):
+            got = gain_got[h]
+            for j in range(2):
+                b = 2 * h + j
+                g_ps = bank("g_ps")
+                for t in range(TILES):
+                    nc.tensor.transpose(g_ps[:, P * t : P * (t + 1)], got[t][:, P * j : P * (j + 1)], ident[:])
+                hid = sb([P, H], BF16, "hid%d" % b)
+                nc.vector.tensor_tensor(hid[:], g_ps[:], inv[b][:], ALU.mult)
+                words = hid[:].bitcast(F32)
+                last = bank("last")
+                for u in range(2):
+                    nc.tensor.transpose(last[:, P * u : P * (u + 1)], words[:, u::2], ident[:])
+                grouped = sb([P, P * 4], BF16, "grouped%d" % b)
+                nc.scalar.copy(
+                    grouped[:].bitcast(F32).rearrange("p (r u) -> p r u", u=2),
+                    last[:, 0 : 2 * P].rearrange("p (u r) -> p r u", u=2),
+                )
+                codes = sb([P, P], U32, "codes%d" % b)
+                plane = sb([P, P], U8, "plane%d" % b)
+                nc.vector.quantize_mx(out=codes[:].bitcast(FP8X4), scales=plane[:], in_=grouped[:])
+                for m in range(N // P):
+                    nc.tensor.matmul_mx(
+                        out=last[:, P * (2 + m) : P * (3 + m)],
+                        lhsT=w3_w[:, 2 * P * m : 2 * P * (m + 1)].bitcast(FP4X4),
+                        lhsT_scale=w3_s[:, 0, P * m : P * (m + 1)],
+                        rhs=codes[:].bitcast(FP8X4),
+                        rhs_scale=plane[:],
+                        start=True,
+                        stop=True,
+                    )
+                res = sb([P, N // P, P], F32, "res%d" % b)
+                nc.scalar.copy(res[:].rearrange("p m r -> p (m r)"), last[:, 2 * P : 4 * P])
+                nc.sync.dma_start(out=out.rearrange("(m p) r -> p m r", p=P)[:, :, P * b : P * (b + 1)], in_=res[:])

@@ -26,6 +26,7 @@ CHUNK = 512
 CHUNKS = S // CHUNK
 HALF = 256
 WINDOW = V + 16
+TREE_WINDOW = U + 16
 KNEE = 11.0
 KNEE_SIGMOID = 1.0 / (1.0 + math.exp(KNEE))
 
@@ -47,60 +48,70 @@ def tile_picked_yentrd_rel_p_kernel(
 
         offs_t = sb([P, S // 16], U16, "offs_t")
         bud_t = sb([P, U // 16], U16, "bud_t")
-        xs_win = reuse.tile([P, T], U8, name="xs_win", align_bytes=64, offset=7680)
-        xw_win = [sb([P, T], I32, "xw_win%d" % o) for o in range(PASSES)]
+        xs_win = reuse.tile([P, T], U8, name="xs_win", align_bytes=64, offset=8 * T)
+        xw_win = [
+            reuse.tile([P, T], I32, name="xw_win%d" % o, align_bytes=64, offset=4 * T * o) for o in range(PASSES)
+        ]
         xs_got = sb([P, S], U8, "xs_got")
         xs_moved = sb([P, S], U8, "xs_moved")
         xw_got = [[sb([P, CHUNK], U32, "xw_got%d_%d" % (o, c)) for c in range(CHUNKS)] for o in range(PASSES)]
         w_w = [
-            reuse.tile([P, PASSES, 2 * H], U8, name="w_w0", align_bytes=64, offset=8768),
+            sb([P, PASSES, 2 * H], U8, "w_w0"),
             sb([P, PASSES, 2 * H], U8, "w_w1"),
         ]
-        w_s = [sb([P, PASSES, H], U8, "w_s%d" % m) for m in range(2)]
-        w3_w = reuse.tile([P, 2 * N], U8, name="w3_w", align_bytes=64, offset=8192)
-        w3_s = sb([P, 1, N], U8, "w3_s")
+        w_s = [
+            reuse.tile([P, PASSES, H], U8, name="w_s0", align_bytes=64, offset=8 * T),
+            sb([P, PASSES, H], U8, "w_s1"),
+        ]
+        w3_w = reuse.tile([P, 1, 2 * N], U8, name="w3_w", align_bytes=64, offset=4 * T + 512)
+        w3_s = reuse.tile([P, 1, N], U8, name="w3_s", align_bytes=64, offset=4 * T + 64)
         cost_t = reuse.tile([P, TILES, U], F32, name="cost_t", align_bytes=64, offset=0)
-        unit_t = reuse.tile([P, TILES], F32, name="unit_t", align_bytes=64, offset=8704)
+        unit_t = reuse.tile([P, TILES], F32, name="unit_t", align_bytes=64, offset=4 * T)
         ident = sb([P, P], F32, "ident")
 
-        s_pair = [sb([P, 2, GROUP, V], F32, "s_pair%d" % t) for t in range(TILES // 2)]
-        s_t = [s_pair[t // 2][:, t % 2] for t in range(TILES)]
+        s_t = [sb([P, GROUP, V], F32, "s_t%d" % t) for t in range(TILES)]
         g_t = [sb([P, GROUP, V], F32, "g_t%d" % t) for t in range(TILES)]
         a_t = [sb([P, GROUP, V + 8], F32, "a_t%d" % t) for t in range(TILES)]
-        over = [sb([P, V], F32, "over%d" % t) for t in range(TILES)]
+        over = [sb([P, V], F32, "over%d" % t) for t in range(2)]
         prod = sb([P, TILES, V], F32, "prod")
         logp = sb([P, TILES, V], F32, "logp")
-        tree_win = [sb([P, WINDOW], F32, "tree_win%d" % t) for t in range(TILES)]
-        gain_win = [sb([P, WINDOW], F32, "gain_win%d" % t) for t in range(TILES)]
+        tree_win = [sb([P, TREE_WINDOW], F32, "tree_win%d" % t) for t in range(TILES)]
+        gain_win = [sb([P, TREE_WINDOW if t < 2 else WINDOW], F32, "gain_win%d" % t) for t in range(TILES)]
 
-        nc.vector.memset(xs_win[:].bitcast(I32), 0)
+        nc.gpsimd.memset(xs_win[:].bitcast(I32), 0)
+        nc.vector.memset(w_s[1][:].bitcast(I32), 0)
+        for t in range(TILES):
+            nc.vector.memset(a_t[t][:, 0, V : V + 8], 0.0)
         nc.vector.memset(xs_moved[:].bitcast(I32), 0)
+        for t in range(TILES):
+            nc.vector.memset(tree_win[t][:, V:TREE_WINDOW], 0.0)
+            nc.vector.memset(gain_win[t][:, V:], 0.0)
 
-        def load_scales(tile, scales):
-            nc.gpsimd.memset(tile[:].bitcast(I32), 0)
+        def load_scales(tile, scales, queue):
             for q in range(4):
-                nc.gpsimd.dma_start(
+                queue.dma_start(
                     out=tile[32 * q : 32 * q + 4].bitcast(I32),
                     in_=scales[:, 4 * q : 4 * q + 4, :].rearrange("o r c -> r o c").bitcast(I32),
                 )
+
+        def load_words(tile, words, rows):
+            nc.sync.dma_start(out=tile[rows].bitcast(I32), in_=words.rearrange("o p c -> p o c")[rows].bitcast(I32))
 
         nc.sync.dma_start(offs_t[:], offs)
         for q in range(4):
             nc.sync.dma_start(
                 out=xs_win[32 * q : 32 * q + 8, :].bitcast(I32), in_=x_scales[:, 4 * q : 4 * q + 4, :].bitcast(I32)
             )
-        for o in range(PASSES):
-            nc.sync.dma_start(out=xw_win[o][:], in_=x_words[o].rearrange("p n t -> p (n t)").bitcast(I32))
-        nc.sync.dma_start(out=w_w[1][:].bitcast(I32), in_=w2_words.rearrange("o p c -> p o c").bitcast(I32))
+        load_words(w_w[1], w2_words, slice(0, 96))
+        nc.sync.dma_start(out=xw_win[0][:], in_=x_words[0].rearrange("p n t -> p (n t)").bitcast(I32))
+        load_words(w_w[1], w2_words, slice(96, P))
+        nc.sync.dma_start(out=xw_win[1][:], in_=x_words[1].rearrange("p n t -> p (n t)").bitcast(I32))
         nc.sync.dma_start(bud_t[:], bud)
-        load_scales(w_s[1], w2_scales)
-        load_scales(w_s[0], w1_scales)
-        load_scales(w3_s, w3_scales)
+        load_words(w_w[0], w1_words, slice(0, P))
+        load_scales(w_s[1], w2_scales, nc.gpsimd)
         make_identity(nc, ident[:])
-        for t in range(TILES):
-            nc.gpsimd.memset(a_t[t][:, 0, V : V + 8], 0.0)
-            nc.gpsimd.memset(tree_win[t][:, V:WINDOW], 0.0)
-            nc.gpsimd.memset(gain_win[t][:, V:WINDOW], 0.0)
+        warm = sb([P, 3], F32, "warm")
+        nc.scalar.activation(warm[:, 0:1], a_t[0][:, 0, V : V + 1], ACT.Sigmoid)
 
         nc.vector.tensor_copy(xs_got[:], xs_win[:].indirect(offs_t[:]))
         for q in range(4):
@@ -112,15 +123,19 @@ def tile_picked_yentrd_rel_p_kernel(
                 cols = slice(c * CHUNK // 16, (c + 1) * CHUNK // 16)
                 nc.vector.tensor_copy(xw_got[o][c][:], xw_win[o][:].bitcast(U32).indirect(offs_t[:, cols]))
 
-        nc.sync.dma_start(out=w_w[0][:].bitcast(I32), in_=w1_words.rearrange("o p c -> p o c").bitcast(I32))
+        nc.vector.memset(w_s[0][:].bitcast(I32), 0)
+        load_scales(w_s[0], w1_scales, nc.sync)
+        nc.sync.dma_start(out=cost_t[:], in_=cost.rearrange("(t p) r -> p t r", p=P))
         with nc.allow_non_contiguous_dma(reason="one value a partition and tile"):
             nc.sync.dma_start(out=unit_t[:], in_=unit.rearrange("(t p) o -> p (t o)", p=P))
-        nc.sync.dma_start(out=cost_t[:], in_=cost.rearrange("(t p) r -> p t r", p=P))
-        nc.sync.dma_start(out=w3_w[:].bitcast(I32), in_=w3_words[0].bitcast(I32))
+        load_words(w3_w, w3_words, slice(0, P))
+        nc.gpsimd.memset(w3_s[:].bitcast(I32), 0)
+        load_scales(w3_s, w3_scales, nc.sync)
 
         def product(m, t, c):
             acc = bank("acc")
-            for o in range(PASSES):
+            order = [0, 1] if (m, c) == (1, 0) and t < 2 else [1, 0]
+            for o in order:
                 x_plane = xs_got if o == 0 else xs_moved
                 nc.tensor.matmul_mx(
                     out=acc[:],
@@ -128,142 +143,163 @@ def tile_picked_yentrd_rel_p_kernel(
                     lhsT_scale=w_s[m][:, o, P * t : P * (t + 1)],
                     rhs=xw_got[o][c][:].bitcast(FP8X4),
                     rhs_scale=x_plane[:, CHUNK * c : CHUNK * (c + 1)],
-                    start=(o == 0),
-                    stop=(o == PASSES - 1),
+                    start=(o == order[0]),
+                    stop=(o == order[-1]),
                 )
             return acc[:].rearrange("p (v d) -> p d v", d=GROUP)
 
-        def entropy(c):
-            vs = slice(P * c, P * (c + 1))
-            en = []
-            for t in range(TILES):
-                en.append(product(1, t, c))
-                nc.scalar.activation(s_t[t][:, :, vs], en[t], ACT.Sigmoid, scale=-1.0)
-            for t in range(TILES):
-                nc.vector.tensor_scalar(over[t][:, vs], en[t][:, 0, :], KNEE, -GROUP * KNEE, ALU.max, ALU.add)
+        def entropy(i):
+            banks = []
+            for c in range(CHUNKS):
+                vs = slice(P * c, P * (c + 1))
+                for t in (2 * i, 2 * i + 1):
+                    en = product(1, t, c)
+                    nc.scalar.activation(s_t[t][:, :, vs], en, ACT.Sigmoid, scale=-1.0)
+                    banks.append(en)
+            return banks
+
+        def add_excess(banks, sums):
             for d in range(1, GROUP):
-                for t in range(TILES):
-                    nc.vector.scalar_tensor_tensor(
-                        over[t][:, vs], en[t][:, d, :], KNEE, over[t][:, vs], ALU.max, ALU.add
-                    )
+                for en, total in zip(banks, sums):
+                    nc.vector.scalar_tensor_tensor(total, en[:, d, :], KNEE, total, ALU.max, ALU.add)
 
         def logit(t, c):
             lg = product(0, t, c)
             nc.scalar.activation(g_t[t][:, :, P * c : P * (c + 1)], lg, ACT.Sigmoid)
 
-        def group_products():
-            for i in range(2):
-                nc.vector.tensor_scalar(
-                    prod[:, 2 * i : 2 * i + 2, :], s_pair[i][:, :, 0, :], KNEE_SIGMOID, None, ALU.max
-                )
+        def group_product(i):
+            for t in (2 * i, 2 * i + 1):
+                nc.vector.tensor_scalar(prod[:, t, :], s_t[t][:, 0, :], KNEE_SIGMOID, None, ALU.max)
             for d in range(1, GROUP):
-                for i in range(2):
-                    both_tiles = prod[:, 2 * i : 2 * i + 2, :]
+                for t in (2 * i, 2 * i + 1):
                     nc.vector.scalar_tensor_tensor(
-                        both_tiles, s_pair[i][:, :, d, :], KNEE_SIGMOID, both_tiles, ALU.max, ALU.mult
+                        prod[:, t, :], s_t[t][:, d, :], KNEE_SIGMOID, prod[:, t, :], ALU.max, ALU.mult
                     )
 
         def gain(t):
             a = a_t[t]
             pair = sb([P, 2, V], F32, "pair%d" % t)
             both = sb([P, 2, V], F32, "both%d" % t)
-            nc.vector.tensor_tensor(a[:, :, 0:V], s_t[t], g_t[t][:], ALU.mult)
+            for first in range(2):
+                nc.vector.tensor_tensor(a[:, first::2, 0:V], s_t[t][:, first::2], g_t[t][:, first::2], ALU.mult)
             nc.vector.tensor_tensor(pair[:, 0, :], a[:, 0, 0:V], a[:, 2, 0:V], ALU.add)
             nc.vector.tensor_tensor(pair[:, 1, :], a[:, 0, 1 : V + 1], a[:, 2, 0:V], ALU.add)
             nc.vector.scalar_tensor_tensor(both[:], a[:, 1::2, 0:V], unit_t[:, t : t + 1], pair[:], ALU.mult, ALU.mult)
             nc.vector.tensor_tensor(gain_win[t][:, 0:V], both[:, 0, :], both[:, 1, :], ALU.add)
 
-        for c in range(CHUNKS):
-            entropy(c)
-        for t in range(TILES):
-            for c in range(CHUNKS):
-                logit(t, c)
-        group_products()
+        def logits(i):
+            for t in (2 * i, 2 * i + 1):
+                for c in range(CHUNKS):
+                    logit(t, c)
+
+        def pieces(tiles):
+            return [tile[:, P * c : P * (c + 1)] for c in range(CHUNKS) for tile in tiles]
+
+        en_first = entropy(0)
+        logits(0)
+        for en, total in zip(en_first, pieces(over)):
+            nc.vector.tensor_scalar(total, en[:, 0, :], KNEE, None, ALU.max)
+        add_excess(en_first, pieces(over))
+        en_second = entropy(1)
+        logits(1)
+        nc.scalar.activation(warm[:, 1:2], g_t[TILES - 1][:, 0, V - 1 : V], ACT.Ln, bias=1.0)
+        for i in range(TILES // 2):
+            group_product(i)
         nc.scalar.activation(logp[:], prod[:], ACT.Ln)
-        for t in range(TILES):
+        nc.scalar.activation(warm[:, 2:3], logp[:, 0, 0:1], ACT.Abs_reciprocal_sqrt, bias=1.0, scale=-1.0)
+        for t in range(2):
             nc.vector.tensor_tensor(tree_win[t][:, 0:V], over[t][:], logp[:, t, :], ALU.subtract)
+        for t in range(2, TILES):
+            banks = en_second[t - 2 :: 2]
+            sums = pieces([tree_win[t]])
+            for en, total, log_piece in zip(banks, sums, pieces([logp[:, t, :]])):
+                nc.vector.scalar_tensor_tensor(total, en[:, 0, :], KNEE, log_piece, ALU.max, ALU.subtract)
+            add_excess(banks, sums)
+        tree_got = []
+        for t in range(TILES):
+            fetched = sb([P, U], F32, "tree_got%d" % t)
+            nc.scalar.activation(
+                fetched[:], tree_win[t][:].indirect(bud_t[:]), ACT.Copy, bias=0.3 - KNEE, scale=1.0 / GROUP
+            )
+            tree_got.append(fetched)
 
-        def bud_cols(h):
-            return bud_t[:, h * HALF // 16 : (h + 1) * HALF // 16]
-
-        den = []
-        for h in range(2):
-            got = []
+        den = [bank("d_ps") for b in range(4)]
+        for b in range(4):
             for t in range(TILES):
-                tree_got = sb([P, HALF], F32, "tree_got%d_%d" % (h, t))
-                nc.scalar.activation(
-                    tree_got[:], tree_win[t][:].indirect(bud_cols(h)), ACT.Copy, bias=0.3, scale=1.0 / GROUP
+                nc.tensor.matmul(
+                    den[b][:, P * t : P * (t + 1)], cost_t[:, t, P * b : P * (b + 1)], ident[:],
+                    start=(t == 0), stop=False, is_transpose=True,
                 )
-                got.append(tree_got)
-            for j in range(2):
-                b = 2 * h + j
-                d_ps = bank("d_ps")
-                for t in range(TILES):
-                    cols = slice(P * t, P * (t + 1))
-                    nc.tensor.matmul(
-                        d_ps[:, cols], cost_t[:, t, P * b : P * (b + 1)], ident[:], start=True, stop=False,
-                        is_transpose=True,
-                    )
-                    nc.tensor.matmul(
-                        d_ps[:, cols], got[t][:, P * j : P * (j + 1)], ident[:], start=False, stop=True,
-                        is_transpose=True,
-                    )
-                den.append(d_ps)
+        for t in range(TILES):
+            for b in range(4):
+                nc.tensor.matmul(
+                    den[b][:, P * t : P * (t + 1)], tree_got[t][:, P * b : P * (b + 1)], ident[:],
+                    start=False, stop=(t == TILES - 1), is_transpose=True,
+                )
 
-        gain_got = [[None] * TILES for h in range(2)]
+        gain_got = [sb([P, U], F32, "gain_got%d" % t) for t in range(TILES)]
         for t in range(TILES):
             gain(t)
-            for h in range(2):
-                fetched = sb([P, HALF], F32, "gain_got%d_%d" % (h, t))
-                if t == 0:
-                    nc.scalar.activation(fetched[:], gain_win[t][:].indirect(bud_cols(h)), ACT.Copy)
-                else:
-                    nc.vector.tensor_copy(fetched[:], gain_win[t][:].indirect(bud_cols(h)))
-                gain_got[h][t] = fetched
+            if t < 2:
+                nc.scalar.activation(gain_got[t][:], gain_win[t][:].indirect(bud_t[:]), ACT.Copy)
+        for h in range(2):
+            bud_half = bud_t[:, h * HALF // 16 : (h + 1) * HALF // 16]
+            for t in range(2, TILES):
+                nc.vector.tensor_copy(gain_got[t][:, HALF * h : HALF * (h + 1)], gain_win[t][:].indirect(bud_half))
+
+        def dealt(bank_tile):
+            return bank_tile[:].rearrange("r (p u e) -> r u p e", u=2, e=2)
+
+        def flat(tile):
+            return tile[:].rearrange("r (u p e) -> r u p e", u=2, e=2)
 
         inv = []
+        sign = []
         for b in range(4):
-            sq = sb([P, H], F32, "sq%d" % b)
-            ra = sb([P, H], F32, "ra%d" % b)
-            q2 = sb([P, H], F32, "q2%d" % b)
+            root = sb([P, H], F32, "root%d" % b)
             w = sb([P, H], F32, "inv%d" % b)
-            nc.scalar.activation(sq[:], den[b][:], ACT.Square)
-            nc.scalar.activation(ra[:], sq[:], ACT.Abs_reciprocal_sqrt)
-            nc.scalar.activation(q2[:], ra[:], ACT.Square)
-            nc.vector.tensor_tensor(w[:], den[b][:], q2[:], ALU.mult)
+            sg = sb([P, H], BF16, "sign%d" % b)
+            nc.scalar.activation(flat(root), dealt(den[b]), ACT.Abs_reciprocal_sqrt)
+            nc.scalar.activation(flat(sg), dealt(den[b]), ACT.Sign)
+            nc.gpsimd.tensor_tensor(w[:], root[:], root[:], ALU.mult)
             inv.append(w)
+            sign.append(sg)
 
-        for h in range(2):
-            got = gain_got[h]
-            for j in range(2):
-                b = 2 * h + j
-                g_ps = bank("g_ps")
-                for t in range(TILES):
-                    nc.tensor.transpose(g_ps[:, P * t : P * (t + 1)], got[t][:, P * j : P * (j + 1)], ident[:])
-                hid = sb([P, H], BF16, "hid%d" % b)
-                nc.vector.tensor_tensor(hid[:], g_ps[:], inv[b][:], ALU.mult)
-                words = hid[:].bitcast(F32)
-                last = bank("last")
-                for u in range(2):
-                    nc.tensor.transpose(last[:, P * u : P * (u + 1)], words[:, u::2], ident[:])
-                grouped = sb([P, P * 4], BF16, "grouped%d" % b)
-                nc.scalar.copy(
-                    grouped[:].bitcast(F32).rearrange("p (r u) -> p r u", u=2),
-                    last[:, 0 : 2 * P].rearrange("p (u r) -> p r u", u=2),
+        hid = []
+        for b in range(4):
+            g_ps = bank("g_ps")
+            rows = slice(P * b, P * (b + 1))
+            for t in range(TILES):
+                nc.tensor.transpose(g_ps[:, P * t : P * (t + 1)], gain_got[t][:, rows], ident[:])
+            size = sb([P, H], BF16, "size%d" % b)
+            signed = sb([P, H], BF16, "hid%d" % b)
+            nc.vector.tensor_tensor(flat(size), dealt(g_ps), flat(inv[b]), ALU.mult)
+            nc.vector.tensor_tensor(signed[:], size[:], sign[b][:], ALU.mult)
+            hid.append(signed)
+
+        for b in range(4):
+            words = hid[b][:].bitcast(F32)
+            last = bank("last")
+            for u in range(2):
+                nc.tensor.transpose(last[:, P * u : P * (u + 1)], words[:, P * u : P * (u + 1)], ident[:])
+            grouped = sb([P, P * 4], BF16, "grouped%d" % b)
+            nc.scalar.copy(
+                grouped[:].bitcast(F32).rearrange("p (r u) -> p r u", u=2),
+                last[:, 0 : 2 * P].rearrange("p (u r) -> p r u", u=2),
+            )
+            codes = sb([P, P], U32, "codes%d" % b)
+            plane = sb([P, P], U8, "plane%d" % b)
+            nc.vector.quantize_mx(out=codes[:].bitcast(FP8X4), scales=plane[:], in_=grouped[:])
+            for m in range(N // P):
+                nc.tensor.matmul_mx(
+                    out=last[:, P * (2 + m) : P * (3 + m)],
+                    lhsT=w3_w[:, 0, 2 * P * m : 2 * P * (m + 1)].bitcast(FP4X4),
+                    lhsT_scale=w3_s[:, 0, P * m : P * (m + 1)],
+                    rhs=codes[:].bitcast(FP8X4),
+                    rhs_scale=plane[:],
+                    start=True,
+                    stop=True,
                 )
-                codes = sb([P, P], U32, "codes%d" % b)
-                plane = sb([P, P], U8, "plane%d" % b)
-                nc.vector.quantize_mx(out=codes[:].bitcast(FP8X4), scales=plane[:], in_=grouped[:])
-                for m in range(N // P):
-                    nc.tensor.matmul_mx(
-                        out=last[:, P * (2 + m) : P * (3 + m)],
-                        lhsT=w3_w[:, 2 * P * m : 2 * P * (m + 1)].bitcast(FP4X4),
-                        lhsT_scale=w3_s[:, 0, P * m : P * (m + 1)],
-                        rhs=codes[:].bitcast(FP8X4),
-                        rhs_scale=plane[:],
-                        start=True,
-                        stop=True,
-                    )
-                res = sb([P, N // P, P], F32, "res%d" % b)
-                nc.scalar.copy(res[:].rearrange("p m r -> p (m r)"), last[:, 2 * P : 4 * P])
-                nc.sync.dma_start(out=out.rearrange("(m p) r -> p m r", p=P)[:, :, P * b : P * (b + 1)], in_=res[:])
+            res = sb([P, N // P, P], F32, "res%d" % b)
+            nc.scalar.copy(res[:].rearrange("p m r -> p (m r)"), last[:, 2 * P : 4 * P])
+            nc.sync.dma_start(out=out.rearrange("(m p) r -> p m r", p=P)[:, :, P * b : P * (b + 1)], in_=res[:])

@@ -76,7 +76,7 @@ def tile_picked_yentrd_rel_p_kernel(
         prod = sb([P, TILES, V], F32, "prod")
         logp = sb([P, TILES, V], F32, "logp")
         tree_win = [sb([P, TREE_WINDOW], F32, "tree_win%d" % t) for t in range(TILES)]
-        gain_win = [sb([P, TREE_WINDOW if t < 2 else WINDOW], F32, "gain_win%d" % t) for t in range(TILES)]
+        gain_win = [sb([P, WINDOW if t else TREE_WINDOW], F32, "gain_win%d" % t) for t in range(TILES)]
 
         nc.gpsimd.memset(xs_win[:].bitcast(I32), 0)
         nc.vector.memset(w_s[1][:].bitcast(I32), 0)
@@ -240,11 +240,11 @@ def tile_picked_yentrd_rel_p_kernel(
         gain_got = [sb([P, U], F32, "gain_got%d" % t) for t in range(TILES)]
         for t in range(TILES):
             gain(t)
-            if t < 2:
+            if t == 0:
                 nc.scalar.activation(gain_got[t][:], gain_win[t][:].indirect(bud_t[:]), ACT.Copy)
         for h in range(2):
             bud_half = bud_t[:, h * HALF // 16 : (h + 1) * HALF // 16]
-            for t in range(2, TILES):
+            for t in range(1, TILES):
                 nc.vector.tensor_copy(gain_got[t][:, HALF * h : HALF * (h + 1)], gain_win[t][:].indirect(bud_half))
 
         def dealt(bank_tile):
@@ -261,7 +261,7 @@ def tile_picked_yentrd_rel_p_kernel(
             sg = sb([P, H], BF16, "sign%d" % b)
             nc.scalar.activation(flat(root), dealt(den[b]), ACT.Abs_reciprocal_sqrt)
             nc.scalar.activation(flat(sg), dealt(den[b]), ACT.Sign)
-            nc.gpsimd.tensor_tensor(w[:], root[:], root[:], ALU.mult)
+            nc.scalar.activation(w[:], root[:], ACT.Square)
             inv.append(w)
             sign.append(sg)
 

import math
from contextlib import ExitStack

import concourse.mybir as mybir
from concourse.masks import make_identity

K, T, S, H, N, V, U = 1024, 2048, 1024, 512, 256, 256, 512
FLOPS = 2 * (2 * K * H * S + H * N * U)

F32 = mybir.dt.float32
BF16 = mybir.dt.bfloat16
I32 = mybir.dt.int32
U32 = mybir.dt.uint32
U16 = mybir.dt.uint16
U8 = mybir.dt.uint8
FP8X4 = mybir.dt.float8_e4m3fn_x4
FP4X4 = mybir.dt.float4_e2m1fn_x4
ALU = mybir.AluOpType
ACT = mybir.ActivationFunctionType

P = 128
PASSES = K // 512
TILES = H // P
GROUP = 4
CHUNK = 512
CHUNKS = S // CHUNK
HALF = 256
WINDOW = V + 16
TREE_WINDOW = U + 16
KNEE = 11.0
KNEE_SIGMOID = 1.0 / (1.0 + math.exp(KNEE))


def tile_picked_yentrd_rel_p_kernel(
    tc, x_words, x_scales, w1_words, w1_scales, w2_words, w2_scales, cost, unit, w3_words, w3_scales, offs, bud, out
):
    nc = tc.nc
    with ExitStack() as ctx:
        keep = ctx.enter_context(tc.tile_pool(name="keep", bufs=1))
        reuse = ctx.enter_context(tc.tile_pool(name="reuse", bufs=1))
        psum = ctx.enter_context(tc.psum_pool(name="psum", bufs=8))

        def sb(shape, dtype, name):
            return keep.tile(shape, dtype, name=name, align_bytes=64)

        def bank(name):
            return psum.tile([P, 512], F32, name=name, tag="bank")

        offs_t = sb([P, S // 16], U16, "offs_t")
        bud_t = sb([P, U // 16], U16, "bud_t")
        xs_win = reuse.tile([P, T], U8, name="xs_win", align_bytes=64, offset=8 * T)
        xw_win = [
            reuse.tile([P, T], I32, name="xw_win%d" % o, align_bytes=64, offset=4 * T * o) for o in range(PASSES)
        ]
        xs_got = sb([P, S], U8, "xs_got")
        xs_moved = sb([P, S], U8, "xs_moved")
        xw_got = [[sb([P, CHUNK], U32, "xw_got%d_%d" % (o, c)) for c in range(CHUNKS)] for o in range(PASSES)]
        w_w = [
            sb([P, PASSES, 2 * H], U8, "w_w0"),
            sb([P, PASSES, 2 * H], U8, "w_w1"),
        ]
        w_s = [
            reuse.tile([P, PASSES, H], U8, name="w_s0", align_bytes=64, offset=8 * T),
            sb([P, PASSES, H], U8, "w_s1"),
        ]
        w3_w = reuse.tile([P, 1, 2 * N], U8, name="w3_w", align_bytes=64, offset=4 * T + 512)
        w3_s = reuse.tile([P, 1, N], U8, name="w3_s", align_bytes=64, offset=4 * T + 64)
        cost_t = reuse.tile([P, TILES, U], F32, name="cost_t", align_bytes=64, offset=0)
        unit_t = reuse.tile([P, TILES], F32, name="unit_t", align_bytes=64, offset=4 * T)
        ident = sb([P, P], F32, "ident")

        s_t = [sb([P, GROUP, V], F32, "s_t%d" % t) for t in range(TILES)]
        g_t = [sb([P, GROUP, V], F32, "g_t%d" % t) for t in range(TILES)]
        a_t = [sb([P, GROUP, V + 8], F32, "a_t%d" % t) for t in range(TILES)]
        over = [sb([P, V], F32, "over%d" % t) for t in range(2)]
        prod = sb([P, TILES, V], F32, "prod")
        logp = sb([P, TILES, V], F32, "logp")
        tree_win = [sb([P, TREE_WINDOW], F32, "tree_win%d" % t) for t in range(TILES)]
        gain_win = [sb([P, WINDOW if t else TREE_WINDOW], F32, "gain_win%d" % t) for t in range(TILES)]

        nc.gpsimd.memset(xs_win[:].bitcast(I32), 0)
        nc.vector.memset(w_s[1][:].bitcast(I32), 0)
        for t in range(TILES):
            nc.vector.memset(a_t[t][:, 0, V : V + 8], 0.0)
        nc.vector.memset(xs_moved[:].bitcast(I32), 0)
        for t in range(TILES):
            nc.vector.memset(tree_win[t][:, V:TREE_WINDOW], 0.0)
            nc.vector.memset(gain_win[t][:, V:], 0.0)

        def load_scales(tile, scales, queue):
            for q in range(4):
                queue.dma_start(
                    out=tile[32 * q : 32 * q + 4].bitcast(I32),
                    in_=scales[:, 4 * q : 4 * q + 4, :].rearrange("o r c -> r o c").bitcast(I32),
                )

        def load_words(tile, words, rows):
            nc.sync.dma_start(out=tile[rows].bitcast(I32), in_=words.rearrange("o p c -> p o c")[rows].bitcast(I32))

        nc.sync.dma_start(offs_t[:], offs)
        for q in range(4):
            nc.sync.dma_start(
                out=xs_win[32 * q : 32 * q + 8, :].bitcast(I32), in_=x_scales[:, 4 * q : 4 * q + 4, :].bitcast(I32)
            )
        load_words(w_w[1], w2_words, slice(0, 96))
        nc.sync.dma_start(out=xw_win[0][:], in_=x_words[0].rearrange("p n t -> p (n t)").bitcast(I32))
        load_words(w_w[1], w2_words, slice(96, P))
        nc.sync.dma_start(out=xw_win[1][:], in_=x_words[1].rearrange("p n t -> p (n t)").bitcast(I32))
        nc.sync.dma_start(bud_t[:], bud)
        load_words(w_w[0], w1_words, slice(0, P))
        load_scales(w_s[1], w2_scales, nc.gpsimd)
        make_identity(nc, ident[:])
        warm = sb([P, 3], F32, "warm")
        nc.scalar.activation(warm[:, 0:1], a_t[0][:, 0, V : V + 1], ACT.Sigmoid)

        nc.vector.tensor_copy(xs_got[:], xs_win[:].indirect(offs_t[:]))
        for q in range(4):
            nc.scalar.dma_start(
                out=xs_moved[32 * q : 32 * q + 4, :].bitcast(I32), in_=xs_got[32 * q + 4 : 32 * q + 8, :].bitcast(I32)
            )
        for o in range(PASSES):
            for c in range(CHUNKS):
                cols = slice(c * CHUNK // 16, (c + 1) * CHUNK // 16)
                nc.vector.tensor_copy(xw_got[o][c][:], xw_win[o][:].bitcast(U32).indirect(offs_t[:, cols]))

        nc.vector.memset(w_s[0][:].bitcast(I32), 0)
        load_scales(w_s[0], w1_scales, nc.sync)
        nc.sync.dma_start(out=cost_t[:], in_=cost.rearrange("(t p) r -> p t r", p=P))
        with nc.allow_non_contiguous_dma(reason="one value a partition and tile"):
            nc.sync.dma_start(out=unit_t[:], in_=unit.rearrange("(t p) o -> p (t o)", p=P))
        load_words(w3_w, w3_words, slice(0, P))
        nc.gpsimd.memset(w3_s[:].bitcast(I32), 0)
        load_scales(w3_s, w3_scales, nc.sync)

        def product(m, t, c):
            acc = bank("acc")
            order = [0, 1] if (m, c) == (1, 0) and t < 2 else [1, 0]
            for o in order:
                x_plane = xs_got if o == 0 else xs_moved
                nc.tensor.matmul_mx(
                    out=acc[:],
                    lhsT=w_w[m][:, o, 2 * P * t : 2 * P * (t + 1)].bitcast(FP4X4),
                    lhsT_scale=w_s[m][:, o, P * t : P * (t + 1)],
                    rhs=xw_got[o][c][:].bitcast(FP8X4),
                    rhs_scale=x_plane[:, CHUNK * c : CHUNK * (c + 1)],
                    start=(o == order[0]),
                    stop=(o == order[-1]),
                )
            return acc[:].rearrange("p (v d) -> p d v", d=GROUP)

        def entropy(i):
            banks = []
            for c in range(CHUNKS):
                vs = slice(P * c, P * (c + 1))
                for t in (2 * i, 2 * i + 1):
                    en = product(1, t, c)
                    nc.scalar.activation(s_t[t][:, :, vs], en, ACT.Sigmoid, scale=-1.0)
                    banks.append(en)
            return banks

        def add_excess(banks, sums):
            for d in range(1, GROUP):
                for en, total in zip(banks, sums):
                    nc.vector.scalar_tensor_tensor(total, en[:, d, :], KNEE, total, ALU.max, ALU.add)

        def logit(t, c):
            lg = product(0, t, c)
            nc.scalar.activation(g_t[t][:, :, P * c : P * (c + 1)], lg, ACT.Sigmoid)

        def group_product(i):
            for t in (2 * i, 2 * i + 1):
                nc.vector.tensor_scalar(prod[:, t, :], s_t[t][:, 0, :], KNEE_SIGMOID, None, ALU.max)
            for d in range(1, GROUP):
                for t in (2 * i, 2 * i + 1):
                    nc.vector.scalar_tensor_tensor(
                        prod[:, t, :], s_t[t][:, d, :], KNEE_SIGMOID, prod[:, t, :], ALU.max, ALU.mult
                    )

        def gain(t):
            a = a_t[t]
            pair = sb([P, 2, V], F32, "pair%d" % t)
            both = sb([P, 2, V], F32, "both%d" % t)
            for first in range(2):
                nc.vector.tensor_tensor(a[:, first::2, 0:V], s_t[t][:, first::2], g_t[t][:, first::2], ALU.mult)
            nc.vector.tensor_tensor(pair[:, 0, :], a[:, 0, 0:V], a[:, 2, 0:V], ALU.add)
            nc.vector.tensor_tensor(pair[:, 1, :], a[:, 0, 1 : V + 1], a[:, 2, 0:V], ALU.add)
            nc.vector.scalar_tensor_tensor(both[:], a[:, 1::2, 0:V], unit_t[:, t : t + 1], pair[:], ALU.mult, ALU.mult)
            nc.vector.tensor_tensor(gain_win[t][:, 0:V], both[:, 0, :], both[:, 1, :], ALU.add)

        def logits(i):
            for t in (2 * i, 2 * i + 1):
                for c in range(CHUNKS):
                    logit(t, c)

        def pieces(tiles):
            return [tile[:, P * c : P * (c + 1)] for c in range(CHUNKS) for tile in tiles]

        en_first = entropy(0)
        logits(0)
        for en, total in zip(en_first, pieces(over)):
            nc.vector.tensor_scalar(total, en[:, 0, :], KNEE, None, ALU.max)
        add_excess(en_first, pieces(over))
        en_second = entropy(1)
        logits(1)
        nc.scalar.activation(warm[:, 1:2], g_t[TILES - 1][:, 0, V - 1 : V], ACT.Ln, bias=1.0)
        for i in range(TILES // 2):
            group_product(i)
        nc.scalar.activation(logp[:], prod[:], ACT.Ln)
        nc.scalar.activation(warm[:, 2:3], logp[:, 0, 0:1], ACT.Abs_reciprocal_sqrt, bias=1.0, scale=-1.0)
        for t in range(2):
            nc.vector.tensor_tensor(tree_win[t][:, 0:V], over[t][:], logp[:, t, :], ALU.subtract)
        for t in range(2, TILES):
            banks = en_second[t - 2 :: 2]
            sums = pieces([tree_win[t]])
            for en, total, log_piece in zip(banks, sums, pieces([logp[:, t, :]])):
                nc.vector.scalar_tensor_tensor(total, en[:, 0, :], KNEE, log_piece, ALU.max, ALU.subtract)
            add_excess(banks, sums)
        tree_got = []
        for t in range(TILES):
            fetched = sb([P, U], F32, "tree_got%d" % t)
            nc.scalar.activation(
                fetched[:], tree_win[t][:].indirect(bud_t[:]), ACT.Copy, bias=0.3 - KNEE, scale=1.0 / GROUP
            )
            tree_got.append(fetched)

        den = [bank("d_ps") for b in range(4)]
        for b in range(4):
            for t in range(TILES):
                nc.tensor.matmul(
                    den[b][:, P * t : P * (t + 1)], cost_t[:, t, P * b : P * (b + 1)], ident[:],
                    start=(t == 0), stop=False, is_transpose=True,
                )
        for t in range(TILES):
            for b in range(4):
                nc.tensor.matmul(
                    den[b][:, P * t : P * (t + 1)], tree_got[t][:, P * b : P * (b + 1)], ident[:],
                    start=False, stop=(t == TILES - 1), is_transpose=True,
                )

        gain_got = [sb([P, U], F32, "gain_got%d" % t) for t in range(TILES)]
        for t in range(TILES):
            gain(t)
            if t == 0:
                nc.scalar.activation(gain_got[t][:], gain_win[t][:].indirect(bud_t[:]), ACT.Copy)
        for h in range(2):
            bud_half = bud_t[:, h * HALF // 16 : (h + 1) * HALF // 16]
            for t in range(1, TILES):
                nc.vector.tensor_copy(gain_got[t][:, HALF * h : HALF * (h + 1)], gain_win[t][:].indirect(bud_half))

        def dealt(bank_tile):
            return bank_tile[:].rearrange("r (p u e) -> r u p e", u=2, e=2)

        def flat(tile):
            return tile[:].rearrange("r (u p e) -> r u p e", u=2, e=2)

        inv = []
        sign = []
        for b in range(4):
            root = sb([P, H], F32, "root%d" % b)
            w = sb([P, H], F32, "inv%d" % b)
            sg = sb([P, H], BF16, "sign%d" % b)
            nc.scalar.activation(flat(root), dealt(den[b]), ACT.Abs_reciprocal_sqrt)
            nc.scalar.activation(flat(sg), dealt(den[b]), ACT.Sign)
            nc.scalar.activation(w[:], root[:], ACT.Square)
            inv.append(w)
            sign.append(sg)

        hid = []
        for b in range(4):
            g_ps = bank("g_ps")
            rows = slice(P * b, P * (b + 1))
            for t in range(TILES):
                nc.tensor.transpose(g_ps[:, P * t : P * (t + 1)], gain_got[t][:, rows], ident[:])
            size = sb([P, H], BF16, "size%d" % b)
            signed = sb([P, H], BF16, "hid%d" % b)
            nc.vector.tensor_tensor(flat(size), dealt(g_ps), flat(inv[b]), ALU.mult)
            nc.vector.tensor_tensor(signed[:], size[:], sign[b][:], ALU.mult)
            hid.append(signed)

        for b in range(4):
            words = hid[b][:].bitcast(F32)
            last = bank("last")
            for u in range(2):
                nc.tensor.transpose(last[:, P * u : P * (u + 1)], words[:, P * u : P * (u + 1)], ident[:])
            grouped = sb([P, P * 4], BF16, "grouped%d" % b)
            nc.scalar.copy(
                grouped[:].bitcast(F32).rearrange("p (r u) -> p r u", u=2),
                last[:, 0 : 2 * P].rearrange("p (u r) -> p r u", u=2),
            )
            codes = sb([P, P], U32, "codes%d" % b)
            plane = sb([P, P], U8, "plane%d" % b)
            nc.vector.quantize_mx(out=codes[:].bitcast(FP8X4), scales=plane[:], in_=grouped[:])
            for m in range(N // P):
                nc.tensor.matmul_mx(
                    out=last[:, P * (2 + m) : P * (3 + m)],
                    lhsT=w3_w[:, 0, 2 * P * m : 2 * P * (m + 1)].bitcast(FP4X4),
                    lhsT_scale=w3_s[:, 0, P * m : P * (m + 1)],
                    rhs=codes[:].bitcast(FP8X4),
                    rhs_scale=plane[:],
                    start=True,
                    stop=True,
                )
            res = sb([P, N // P, P], F32, "res%d" % b)
            nc.scalar.copy(res[:].rearrange("p m r -> p (m r)"), last[:, 2 * P : 4 * P])
            nc.sync.dma_start(out=out.rearrange("(m p) r -> p m r", p=P)[:, :, P * b : P * (b + 1)], in_=res[:])
